import numpy as np
import ml_dtypes


def mxq(x, axis, fmt="e4m3"):
    dtype, down = {"e4m3": (ml_dtypes.float8_e4m3fn, 7), "e5m2": (ml_dtypes.float8_e5m2, 14)}[fmt]
    v = np.moveaxis(np.asarray(x, np.float32).astype(ml_dtypes.bfloat16).astype(np.float64), axis, -1)
    blocks = v.reshape(v.shape[:-1] + (-1, 32))
    amax = np.abs(blocks).max(-1, keepdims=True)
    byte = np.maximum(np.where(amax > 0, np.frexp(amax)[1] - 1 + 127, 0) - down, 1)
    scale = np.exp2(byte - 127.0)
    codes = (blocks / scale).astype(np.float32).astype(dtype).astype(np.float64)
    return np.moveaxis((codes * scale).reshape(v.shape), -1, axis)


WIDE = False


def mx_kscale(k):
    if not WIDE:
        return np.ones(k)
    levels = np.array([10, -10, 5, -5, 0])
    if k % 512:
        return np.exp2(np.random.permutation(np.resize(levels, k // 32))).repeat(32)
    a = np.empty((k // 512, 16))
    for p in range(k // 512):
        a[p, :8] = np.random.permutation(np.resize(levels, 8))
        for g in range(8):
            far = levels[np.abs(levels - a[p, g]) >= 10]
            a[p, g + 8] = far[np.random.randint(len(far))]
    return np.exp2(a.ravel()).repeat(32)


def f64(x):
    return np.asarray(x).astype(np.float64)


def striped(idx):
    return np.tile(idx.reshape(-1, 16).T, (8, 1)).astype(np.uint16)


def unstriped(offs):
    return offs[:16].T.reshape(-1).astype(np.int64)


E2M1 = np.array([0.0, 0.5, 1.0, 1.5, 2.0, 3.0, 4.0, 6.0, -0.0, -0.5, -1.0, -1.5, -2.0, -3.0, -4.0, -6.0])


def pack_weight(w, fmt):
    k, n = w.shape
    w = f64(np.asarray(w, np.float32).astype(ml_dtypes.bfloat16)).reshape(k // 32, 32, n)
    amax = np.abs(w).max(1)
    if fmt == "e4m3":
        byte = np.frexp(amax)[1] - 1 + 127 - 7
    else:
        mant, ex = np.frexp(amax / 6.0)
        byte = np.where(mant > 0.5, ex, ex - 1) + 127
    byte = np.clip(np.where(amax > 0, byte, 1), 1, 254)
    scaled = (w * np.exp2(127.0 - byte)[:, None, :]).reshape(k, n).astype(np.float32)
    by_word = np.ascontiguousarray(scaled.reshape(k // 512, 128, 4, n).transpose(0, 1, 3, 2))
    if fmt == "e4m3":
        words = by_word.astype(ml_dtypes.float8_e4m3fn).view(np.uint8)
    else:
        c = by_word.astype(ml_dtypes.float4_e2m1fn).view(np.uint8) & 0xF
        words = (c[..., 0::2] | (c[..., 1::2] << 4)).reshape(k // 512, 128, 2 * n)
    return np.ascontiguousarray(words), np.ascontiguousarray(byte.astype(np.uint8).reshape(k // 512, 16, n))


def unpack_weight(words, scales, fmt):
    g, _, n = scales.shape
    words = np.ascontiguousarray(words).reshape(g, 128, n, -1)
    if fmt == "e4m3":
        vals = words.view(ml_dtypes.float8_e4m3fn).astype(np.float64)
    else:
        nib = np.empty((g, 128, n, 4), np.uint8)
        nib[..., 0::2] = words & 0xF
        nib[..., 1::2] = words >> 4
        vals = E2M1[nib]
    vals = vals * np.repeat(np.exp2(scales.astype(np.float64) - 127.0), 8, axis=1)[..., None]
    return vals.transpose(0, 1, 3, 2).reshape(g * 512, n)


def gelu(v):
    return 0.5 * v * (1.0 + np.tanh(np.sqrt(2.0 / np.pi) * (v + 0.044715 * v**3)))


def bf(x):
    return np.asarray(x, np.float32).astype(ml_dtypes.bfloat16)


def planes(Y):
    n, m = Y.shape
    b = f64(bf(Y)).reshape(n // 32, 32, m)
    amax = np.abs(b).max(1)
    byte = np.clip(np.where(amax > 0, np.frexp(amax)[1] - 1 + 127 - 7, 1), 1, 254)
    codes = (b * np.exp2(127.0 - byte)[:, None, :]).reshape(n, m).astype(np.float32).astype(ml_dtypes.float8_e4m3fn).view(np.uint8)
    words = codes.reshape(n // 512, 128, 4, m).transpose(0, 1, 3, 2)
    return np.ascontiguousarray(words), np.ascontiguousarray(byte.astype(np.uint8).reshape(n // 512, 16, m))


K, R, H, N, T, S = 1024, 512, 1024, 512, 4096, 1024

def setup_inputs():
    n = np.random.standard_normal
    s = mx_kscale(K)[:, None]
    u1 = mx_kscale(R)[:, None]
    u2 = mx_kscale(H)[:, None]
    d = {}
    d["tab_words"], d["tab_scales"] = pack_weight(n((K, T)) * s, "e4m3")
    d["offs"] = striped(np.random.permutation(T)[:S])
    d["xs_words"], d["xs_scales"] = pack_weight(n((K, S)) * s, "e4m3")
    d["w1"] = (1.2 * n((K, R)) / K**0.5 / s).astype(np.float32)
    d["b1"] = (0.6 * n(R)).astype(np.float32)
    d["gain"] = (np.exp(0.3 * n(R)) * u1[:, 0]).astype(np.float32)
    d["w2_words"], d["w2_scales"] = pack_weight(1.4 * n((R, H)) / R**0.5 / u1 * u2.T, "e2m1")
    d["wx"] = (n((K, H)) / K**0.5 / s * u2.T).astype(np.float32)
    d["w3"] = (n((H, N)) / H**0.5 / u2 * np.exp(0.8 * n(N))).astype(np.float32)
    return d

def reference(tab_words, tab_scales, offs, xs_words, xs_scales, w1, b1, gain, w2_words, w2_scales, wx, w3):
    v = unpack_weight(tab_words, tab_scales, "e4m3")[:, unstriped(offs)]
    xs = unpack_weight(xs_words, xs_scales, "e4m3")
    w2 = unpack_weight(w2_words, w2_scales, "e2m1")
    p = (mxq(f64(w1), 0, "e4m3").T @ v) + f64(b1)[:, None]
    h = np.tanh(p) * f64(gain)[:, None]
    a = w2.T @ mxq(h, 0, "e4m3")
    b = mxq(f64(wx), 0, "e4m3").T @ xs
    z = np.minimum(a, b)
    y = mxq(f64(w3), 0, "e4m3").T @ mxq(z, 0, "e4m3")
    words, scales = planes(y)
    return y, words, scales

@@ -1,0 +1,311 @@
+from contextlib import ExitStack
+
+import concourse.mybir as mybir
+
+K, R, H, N, T, S = 1024, 512, 1024, 512, 4096, 1024
+FLOPS = 2 * S * (K * R + R * H + K * H + H * N)
+
+F32 = mybir.dt.float32
+BF16 = mybir.dt.bfloat16
+I32 = mybir.dt.int32
+U32 = mybir.dt.uint32
+U16 = mybir.dt.uint16
+U8 = mybir.dt.uint8
+FP8X4 = mybir.dt.float8_e4m3fn_x4
+FP4X4 = mybir.dt.float4_e2m1fn_x4
+ACT = mybir.ActivationFunctionType
+ALU = mybir.AluOpType
+
+P = 128
+PACK = 4
+KP = P * PACK
+HALF = 512
+QUARTER = 256
+CH = 128
+NCH = S // CH
+W1_SCALAR_M = 40
+WX_SCALAR_M = 64
+PARK_AHEAD = 3
+VECTOR_ROUNDS_FROM = 6
+
+
+def tile_list_mask_pressure_planner_kernel(
+    tc, tab_words, tab_scales, offs, xs_words, xs_scales, w1, b1, gain, w2_words, w2_scales, wx, w3, out_0, out_1, out_2
+):
+    nc = tc.nc
+    with ExitStack() as ctx:
+        keep = ctx.enter_context(tc.tile_pool(name="keep", bufs=1))
+        ring = ctx.enter_context(tc.tile_pool(name="ring", bufs=2))
+        psum = ctx.enter_context(tc.psum_pool(name="psum", bufs=4))
+
+        def words_of(dram, a):
+            return dram[a].rearrange("p n t -> p (n t)").bitcast(I32)
+
+        def rows_of(w, a, g):
+            return w[a * KP : (a + 1) * KP, g * KP : (g + 1) * KP].rearrange("(p j) c -> p j c", j=PACK)
+
+        def load_scale_rows(name, dram, passes, width):
+            plane = keep.tile([P, width], U8, name=name, align_bytes=64)
+            nc.vector.memset(plane[:].bitcast(I32), 0)
+            for q in range(4):
+                nc.sync.dma_start(
+                    plane[32 * q : 32 * q + 4 * passes, :].bitcast(I32), dram[:, 4 * q : 4 * q + 4, :].bitcast(I32)
+                )
+            return plane
+
+        offsets = keep.tile([P, S // 16], U16, name="offsets")
+        nc.sync.dma_start(offsets[:], offs)
+        w2_raw = keep.tile([P, 2 * H], U8, name="w2_raw")
+        nc.sync.dma_start(w2_raw[:].bitcast(I32), w2_words[0].bitcast(I32))
+        tab_s = load_scale_rows("tab_s", tab_scales, 2, T)
+        tab_w = [keep.tile([P, T], I32, name="tab_w%d" % a) for a in range(2)]
+        w1_raw = [ring.tile([P, PACK, KP], F32, name="w1_raw%d" % a, tag="w13") for a in range(2)]
+        nc.sync.dma_start(tab_w[0][:], words_of(tab_words, 0))
+        w2_s_raw = load_scale_rows("w2_s_raw", w2_scales, 1, H)
+        nc.sync.dma_start(w1_raw[0][:], rows_of(w1, 0, 0))
+        nc.sync.dma_start(tab_w[1][:], words_of(tab_words, 1))
+        nc.sync.dma_start(w1_raw[1][:], rows_of(w1, 1, 0))
+        wx_raw = {}
+        xs_w = [keep.tile([P, S], I32, name="xs_w%d" % a, align_bytes=64) for a in range(2)]
+        for g in range(2):
+            for a in range(2):
+                wx_raw[a, g] = keep.tile([P, PACK, KP], F32, name="wx_raw%d%d" % (a, g))
+                nc.sync.dma_start(wx_raw[a, g][:], rows_of(wx, a, g))
+            if g == 0:
+                nc.sync.dma_start(xs_w[0][:], words_of(xs_words, 0))
+                xs_s = load_scale_rows("xs_s", xs_scales, 2, S)
+                nc.sync.dma_start(xs_w[1][:], words_of(xs_words, 1))
+        w3_raw = [ring.tile([P, PACK, KP], F32, name="w3_raw%d" % a, tag="w13") for a in range(2)]
+
+        b1_t = keep.tile([P, PACK], F32, name="b1_t")
+        gain_t = keep.tile([P, PACK], F32, name="gain_t")
+        nc.gpsimd.dma_start(b1_t[:], b1.rearrange("(p t) -> p t", t=PACK))
+        nc.gpsimd.dma_start(gain_t[:], gain.rearrange("(p t) -> p t", t=PACK))
+
+        warm = keep.tile([P, 8], F32, name="warm")
+        nc.vector.memset(warm[:], 0.0)
+        warm_out = keep.tile([P, 8], F32, name="warm_out")
+        nc.scalar.activation(out=warm_out[:], in_=warm[:], func=ACT.Tanh)
+
+        v_w = [keep.tile([P, S], U32, name="v_w%d" % a, align_bytes=64) for a in range(2)]
+        v_s = keep.tile([P, S], U8, name="v_s", align_bytes=64)
+
+        def deal(raw, name, scalar_m):
+            grouped = ring.tile([P, PACK * KP], BF16, name=name, tag="grouped", align_bytes=64, bufs=3)
+            dst = grouped[:].rearrange("p (t m j) -> p m j t", t=PACK, j=PACK)
+            src = raw[:].rearrange("p j (m t) -> p m j t", t=PACK)
+            if scalar_m > 0:
+                nc.scalar.copy(out=dst[:, :scalar_m], in_=src[:, :scalar_m])
+            if scalar_m < P:
+                nc.vector.tensor_copy(out=dst[:, scalar_m:], in_=src[:, scalar_m:])
+            return grouped
+
+        def quantize(src, name):
+            width = src.shape[1] // PACK
+            codes = keep.tile([P, width], U32, name=name + "_w", align_bytes=64)
+            scales = keep.tile([P, width], U8, name=name + "_s", align_bytes=64)
+            nc.vector.quantize_mx(out=codes[:].bitcast(FP8X4), scales=scales[:], in_=src)
+            return codes, scales
+
+        w2_w = keep.tile([P, 2 * H], U8, name="w2_w", align_bytes=64)
+        w2_s = keep.tile([P, H], U8, name="w2_s", align_bytes=64)
+        nc.vector.tensor_copy(
+            out=w2_w[:].rearrange("p (g t q b) -> p g t q b", g=2, t=PACK, b=2),
+            in_=w2_raw[:].rearrange("p (g q t b) -> p g t q b", g=2, t=PACK, b=2),
+        )
+        nc.vector.tensor_copy(out=v_s[:], in_=tab_s[:].indirect(offsets[:]))
+        nc.vector.tensor_copy(out=v_w[0][:], in_=tab_w[0][:].bitcast(U32).indirect(offsets[:]))
+        nc.vector.tensor_copy(
+            out=w2_s[:].rearrange("p (g t q) -> p g t q", g=2, t=PACK),
+            in_=w2_s_raw[:].rearrange("p (g q t) -> p g t q", g=2, t=PACK),
+        )
+
+        w1_q = {}
+        w1_g0 = deal(w1_raw[0], "w1_g0", P)
+        for u in range(2):
+            w1_q[0, u] = quantize(w1_g0[:, u * 2 * KP : (u + 1) * 2 * KP], "w1_0%d" % u)
+        nc.vector.tensor_copy(out=v_w[1][:], in_=tab_w[1][:].bitcast(U32).indirect(offsets[:]))
+        w1_g1 = deal(w1_raw[1], "w1_g1", W1_SCALAR_M)
+        for u in range(2):
+            w1_q[1, u] = quantize(w1_g1[:, u * 2 * KP : (u + 1) * 2 * KP], "w1_1%d" % u)
+        for a in range(2):
+            nc.sync.dma_start(w3_raw[a][:], rows_of(w3, a, 0))
+
+
+        p_bank = {}
+        for hf in range(2):
+            for t in range(PACK):
+                p_bank[hf, t] = psum.tile([P, HALF], F32, name="p%d%d" % (hf, t), tag="bank_s" if hf == 0 else "bank_v")
+        for hf in range(2):
+            cols = slice(hf * HALF, (hf + 1) * HALF)
+            for a in range(2):
+                for t in range(PACK):
+                    m = slice(t % 2 * P, (t % 2 + 1) * P)
+                    nc.tensor.matmul_mx(
+                        out=p_bank[hf, t][:],
+                        lhsT=w1_q[a, t // 2][0][:, m].bitcast(FP8X4),
+                        lhsT_scale=w1_q[a, t // 2][1][:, m],
+                        rhs=v_w[a][:, cols].bitcast(FP8X4),
+                        rhs_scale=v_s[4 * a : P, cols],
+                        start=(a == 0),
+                        stop=(a == 1),
+                    )
+
+        def tanh_half(hf):
+            th = ring.tile([P, PACK, HALF], F32, name="th%d" % hf, tag="th_y")
+            for t in range(PACK):
+                nc.scalar.activation(out=th[:, t, :], in_=p_bank[hf, t][:], func=ACT.Tanh, bias=b1_t[:, t : t + 1])
+            return th
+
+        def gain_quarter(qt):
+            hb = ring.tile([P, PACK * QUARTER], BF16, name="hb%d" % qt, tag="hb", align_bytes=64, bufs=3)
+            cols = slice(qt % 2 * QUARTER, (qt % 2 + 1) * QUARTER)
+            nc.vector.tensor_tensor(
+                out=hb[:].rearrange("p (c i t) -> p c t i", i=4, t=PACK),
+                in0=th[qt // 2][:, :, cols].rearrange("p t (c i) -> p c t i", i=4),
+                in1=gain_t[:].unsqueeze(1).unsqueeze(3).to_broadcast([P, QUARTER // 4, PACK, 4]),
+                op=ALU.mult,
+            )
+            return hb
+
+        def product_a(g, c, tag):
+            bank = psum.tile([P, PACK, CH], F32, name="a%d%d" % (g, c), tag=tag)
+            codes, scales = h_q[c * CH // QUARTER]
+            cols = slice(c * CH % QUARTER, c * CH % QUARTER + CH)
+            for t in range(PACK):
+                s = g * PACK + t
+                nc.tensor.matmul_mx(
+                    out=bank[:, t, :],
+                    lhsT=w2_w[:, 2 * s * P : 2 * (s + 1) * P].bitcast(FP4X4),
+                    lhsT_scale=w2_s[:, s * P : (s + 1) * P],
+                    rhs=codes[:, cols].bitcast(FP8X4),
+                    rhs_scale=scales[:, cols],
+                    start=True,
+                    stop=True,
+                )
+            return bank
+
+        def product_b(g, c, tag):
+            bank = psum.tile([P, PACK, CH], F32, name="b%d%d" % (g, c), tag=tag)
+            cols = slice(c * CH, (c + 1) * CH)
+            for t in range(PACK):
+                m = slice(t * P, (t + 1) * P)
+                for a in range(2):
+                    nc.tensor.matmul_mx(
+                        out=bank[:, t, :],
+                        lhsT=wx_q[a, g][0][:, m].bitcast(FP8X4),
+                        lhsT_scale=wx_q[a, g][1][:, m],
+                        rhs=xs_w[a][:, cols].bitcast(FP8X4),
+                        rhs_scale=xs_s[4 * a : P, cols],
+                        start=(a == 0),
+                        stop=(a == 1),
+                    )
+            return bank
+
+        def park(bank, g, c):
+            held = keep.tile([P, PACK * CH], F32, name="held%d%d" % (g, c))
+            nc.scalar.copy(out=held[:].rearrange("p (n t) -> p n t", t=PACK), in_=bank[:].rearrange("p t n -> p n t"))
+            return held
+
+        def lower(bank, parked, zb, g):
+            nc.vector.tensor_tensor(
+                out=zb[:, g, :].rearrange("p (n t) -> p n t", t=PACK),
+                in0=bank[:].rearrange("p t n -> p n t"),
+                in1=parked[:].rearrange("p (n t) -> p n t", t=PACK),
+                op=ALU.min,
+            )
+
+        wx_q = {}
+        h_q = {}
+        th = [tanh_half(0), tanh_half(1)]
+        wx_g = deal(wx_raw[0, 0], "wx_g00", 0)
+        wx_q[0, 0] = quantize(wx_g[:], "wx00")
+        hb0 = gain_quarter(0)
+        wx_g = deal(wx_raw[1, 0], "wx_g10", WX_SCALAR_M)
+        h_q[0] = quantize(hb0[:], "h0")
+        hb1 = gain_quarter(1)
+        wx_q[1, 0] = quantize(wx_g[:], "wx10")
+        h_q[1] = quantize(hb1[:], "h1")
+        hb2 = gain_quarter(2)
+        wx_g = deal(wx_raw[0, 1], "wx_g01", WX_SCALAR_M)
+        h_q[2] = quantize(hb2[:], "h2")
+        hb3 = gain_quarter(3)
+        wx_q[0, 1] = quantize(wx_g[:], "wx01")
+        h_q[3] = quantize(hb3[:], "h3")
+        wx_g = deal(wx_raw[1, 1], "wx_g11", 0)
+        wx_q[1, 1] = quantize(wx_g[:], "wx11")
+
+        held = {}
+
+        def park_chunk(c):
+            held[0, c] = park(product_b(0, c, "bank_s"), 0, c)
+            held[1, c] = park(product_a(1, c, "bank_s"), 1, c)
+
+        def lower_chunk(c):
+            zb = ring.tile([P, 2, PACK * CH], BF16, name="zb%d" % c, tag="zb", align_bytes=64, bufs=3)
+            lower(product_a(0, c, "bank_v"), held[0, c], zb, 0)
+            lower(product_b(1, c, "bank_v"), held[1, c], zb, 1)
+            return zb
+
+        for c in range(PARK_AHEAD):
+            park_chunk(c)
+        w3_q = [quantize(deal(w3_raw[a], "w3_g%d" % a, P)[:], "w3_%d" % a) for a in range(2)]
+
+        y_w = keep.tile([P, S], U32, name="y_w", align_bytes=64)
+        y_s = keep.tile([P, S], U8, name="y_s", align_bytes=64)
+        out_rows = out_0.rearrange("(p t) s -> p t s", t=PACK)
+        out_words = words_of(out_1, 0)
+
+        def finish(c):
+            cols = slice(c * CH, (c + 1) * CH)
+            bank = psum.tile([P, PACK, CH], F32, name="y%d" % c, tag="bank_s")
+            for t in range(PACK):
+                m = slice(t * P, (t + 1) * P)
+                for g in range(2):
+                    nc.tensor.matmul_mx(
+                        out=bank[:, t, :],
+                        lhsT=w3_q[g][0][:, m].bitcast(FP8X4),
+                        lhsT_scale=w3_q[g][1][:, m],
+                        rhs=z_q[c][0][:, g * CH : (g + 1) * CH].bitcast(FP8X4),
+                        rhs_scale=z_q[c][1][:, g * CH : (g + 1) * CH],
+                        start=(g == 0),
+                        stop=(g == 1),
+                    )
+            yb = ring.tile([P, PACK * CH], BF16, name="yb%d" % c, tag="yb", align_bytes=64, bufs=3)
+            y32 = ring.tile([P, PACK, CH], F32, name="y32_%d" % c, tag="y32", bufs=4)
+            if c < VECTOR_ROUNDS_FROM:
+                nc.scalar.copy(out=yb[:].rearrange("p (n t) -> p n t", t=PACK), in_=bank[:].rearrange("p t n -> p n t"))
+                nc.scalar.copy(out=y32[:], in_=bank[:])
+            else:
+                nc.scalar.copy(out=y32[:], in_=bank[:])
+                nc.vector.tensor_copy(
+                    out=yb[:].rearrange("p (c i t) -> p c t i", i=4, t=PACK),
+                    in_=y32[:].rearrange("p t (c i) -> p c t i", i=4),
+                )
+            nc.sync.dma_start(out_rows[:, :, cols], y32[:])
+            return yb
+
+        def finish_planes(c, yb):
+            cols = slice(c * CH, (c + 1) * CH)
+            nc.vector.quantize_mx(out=y_w[:, cols].bitcast(FP8X4), scales=y_s[:, cols], in_=yb[:])
+            if c % 2 == 1:
+                both = slice((c - 1) * CH, (c + 1) * CH)
+                nc.sync.dma_start(out_words[:, both], y_w[:, both].bitcast(I32))
+
+        zbs = {}
+        z_q = {}
+        ybs = {}
+        for c in range(NCH + 4):
+            if c < NCH:
+                zbs[c] = lower_chunk(c)
+            if 1 <= c <= NCH:
+                z_q[c - 1] = quantize(zbs[c - 1][:].rearrange("p g w -> p (g w)"), "z%d" % (c - 1))
+            if 2 <= c < NCH + 2:
+                ybs[c - 2] = finish(c - 2)
+            if c + PARK_AHEAD < NCH:
+                park_chunk(c + PARK_AHEAD)
+            if c >= 4:
+                finish_planes(c - 4, ybs[c - 4])
+        for q in range(4):
+            queue = nc.sync if q % 2 == 0 else nc.scalar
+            queue.dma_start(out_2[0, 4 * q : 4 * q + 4, :].bitcast(I32), y_s[32 * q : 32 * q + 4, :].bitcast(I32))

@@ -25,7 +25,7 @@ CH = 128
 NCH = S // CH
 W1_SCALAR_M = 40
 WX_SCALAR_M = 64
-PARK_AHEAD = 3
+PARK_AHEAD = 5
 VECTOR_ROUNDS_FROM = 6
 
 
@@ -57,12 +57,12 @@ def tile_list_mask_pressure_planner_kernel(
         nc.sync.dma_start(offsets[:], offs)
         w2_raw = keep.tile([P, 2 * H], U8, name="w2_raw")
         nc.sync.dma_start(w2_raw[:].bitcast(I32), w2_words[0].bitcast(I32))
-        tab_s = load_scale_rows("tab_s", tab_scales, 2, T)
         tab_w = [keep.tile([P, T], I32, name="tab_w%d" % a) for a in range(2)]
         w1_raw = [ring.tile([P, PACK, KP], F32, name="w1_raw%d" % a, tag="w13") for a in range(2)]
         nc.sync.dma_start(tab_w[0][:], words_of(tab_words, 0))
-        w2_s_raw = load_scale_rows("w2_s_raw", w2_scales, 1, H)
+        tab_s = load_scale_rows("tab_s", tab_scales, 2, T)
         nc.sync.dma_start(w1_raw[0][:], rows_of(w1, 0, 0))
+        w2_s_raw = load_scale_rows("w2_s_raw", w2_scales, 1, H)
         nc.sync.dma_start(tab_w[1][:], words_of(tab_words, 1))
         nc.sync.dma_start(w1_raw[1][:], rows_of(w1, 1, 0))
         wx_raw = {}
@@ -113,8 +113,8 @@ def tile_list_mask_pressure_planner_kernel(
             out=w2_w[:].rearrange("p (g t q b) -> p g t q b", g=2, t=PACK, b=2),
             in_=w2_raw[:].rearrange("p (g q t b) -> p g t q b", g=2, t=PACK, b=2),
         )
-        nc.vector.tensor_copy(out=v_s[:], in_=tab_s[:].indirect(offsets[:]))
         nc.vector.tensor_copy(out=v_w[0][:], in_=tab_w[0][:].bitcast(U32).indirect(offsets[:]))
+        nc.vector.tensor_copy(out=v_s[:], in_=tab_s[:].indirect(offsets[:]))
         nc.vector.tensor_copy(
             out=w2_s[:].rearrange("p (g t q) -> p g t q", g=2, t=PACK),
             in_=w2_s_raw[:].rearrange("p (g q t) -> p g t q", g=2, t=PACK),
@@ -249,7 +249,7 @@ def tile_list_mask_pressure_planner_kernel(
 
         for c in range(PARK_AHEAD):
             park_chunk(c)
-        w3_q = [quantize(deal(w3_raw[a], "w3_g%d" % a, P)[:], "w3_%d" % a) for a in range(2)]
+        w3_q = [quantize(deal(w3_raw[a], "w3_g%d" % a, P if a == 0 else WX_SCALAR_M)[:], "w3_%d" % a) for a in range(2)]
 
         y_w = keep.tile([P, S], U32, name="y_w", align_bytes=64)
         y_s = keep.tile([P, S], U8, name="y_s", align_bytes=64)

@@ -19,14 +19,19 @@ ALU = mybir.AluOpType
 P = 128
 PACK = 4
 KP = P * PACK
+QUADRANTS = 4
 HALF = 512
 QUARTER = 256
-CH = 128
-NCH = S // CH
-W1_SCALAR_M = 40
-WX_SCALAR_M = 64
+CHUNK = 128
+CHUNKS = S // CHUNK
+LINE = 4
+
+W1_LAST_SCALAR_GROUPS = 40
+SHARED_SCALAR_GROUPS = 64
 PARK_AHEAD = 5
-VECTOR_ROUNDS_FROM = 6
+PRODUCT_LAG = 2
+PLANES_LAG = 4
+VECTOR_WEAVES_FROM = 6
 
 
 def tile_list_mask_pressure_planner_kernel(
@@ -47,7 +52,7 @@ def tile_list_mask_pressure_planner_kernel(
         def load_scale_rows(name, dram, passes, width):
             plane = keep.tile([P, width], U8, name=name, align_bytes=64)
             nc.vector.memset(plane[:].bitcast(I32), 0)
-            for q in range(4):
+            for q in range(QUADRANTS):
                 nc.sync.dma_start(
                     plane[32 * q : 32 * q + 4 * passes, :].bitcast(I32), dram[:, 4 * q : 4 * q + 4, :].bitcast(I32)
                 )
@@ -58,47 +63,37 @@ def tile_list_mask_pressure_planner_kernel(
         w2_raw = keep.tile([P, 2 * H], U8, name="w2_raw")
         nc.sync.dma_start(w2_raw[:].bitcast(I32), w2_words[0].bitcast(I32))
         tab_w = [keep.tile([P, T], I32, name="tab_w%d" % a) for a in range(2)]
-        w1_raw = [ring.tile([P, PACK, KP], F32, name="w1_raw%d" % a, tag="w13") for a in range(2)]
+        w1_raw = [ring.tile([P, PACK, KP], F32, name="w1_raw%d" % a, tag="w1_then_w3") for a in range(2)]
         nc.sync.dma_start(tab_w[0][:], words_of(tab_words, 0))
         tab_s = load_scale_rows("tab_s", tab_scales, 2, T)
         nc.sync.dma_start(w1_raw[0][:], rows_of(w1, 0, 0))
         w2_s_raw = load_scale_rows("w2_s_raw", w2_scales, 1, H)
         nc.sync.dma_start(tab_w[1][:], words_of(tab_words, 1))
         nc.sync.dma_start(w1_raw[1][:], rows_of(w1, 1, 0))
+        wx_tiles = [(a, g) for g in range(2) for a in range(2)]
         wx_raw = {}
         xs_w = [keep.tile([P, S], I32, name="xs_w%d" % a, align_bytes=64) for a in range(2)]
-        for g in range(2):
-            for a in range(2):
-                wx_raw[a, g] = keep.tile([P, PACK, KP], F32, name="wx_raw%d%d" % (a, g))
-                nc.sync.dma_start(wx_raw[a, g][:], rows_of(wx, a, g))
-            if g == 0:
+        for a, g in wx_tiles:
+            wx_raw[a, g] = keep.tile([P, PACK, KP], F32, name="wx_raw%d%d" % (a, g))
+            nc.sync.dma_start(wx_raw[a, g][:], rows_of(wx, a, g))
+            if (a, g) == (1, 0):
                 nc.sync.dma_start(xs_w[0][:], words_of(xs_words, 0))
                 xs_s = load_scale_rows("xs_s", xs_scales, 2, S)
                 nc.sync.dma_start(xs_w[1][:], words_of(xs_words, 1))
-        w3_raw = [ring.tile([P, PACK, KP], F32, name="w3_raw%d" % a, tag="w13") for a in range(2)]
-
         b1_t = keep.tile([P, PACK], F32, name="b1_t")
         gain_t = keep.tile([P, PACK], F32, name="gain_t")
         nc.gpsimd.dma_start(b1_t[:], b1.rearrange("(p t) -> p t", t=PACK))
         nc.gpsimd.dma_start(gain_t[:], gain.rearrange("(p t) -> p t", t=PACK))
 
-        warm = keep.tile([P, 8], F32, name="warm")
-        nc.vector.memset(warm[:], 0.0)
-        warm_out = keep.tile([P, 8], F32, name="warm_out")
-        nc.scalar.activation(out=warm_out[:], in_=warm[:], func=ACT.Tanh)
-
-        v_w = [keep.tile([P, S], U32, name="v_w%d" % a, align_bytes=64) for a in range(2)]
-        v_s = keep.tile([P, S], U8, name="v_s", align_bytes=64)
-
-        def deal(raw, name, scalar_m):
-            grouped = ring.tile([P, PACK * KP], BF16, name=name, tag="grouped", align_bytes=64, bufs=3)
-            dst = grouped[:].rearrange("p (t m j) -> p m j t", t=PACK, j=PACK)
+        def deal(raw, name, scalar_groups):
+            dealt = ring.tile([P, PACK * KP], BF16, name=name, tag="dealt", align_bytes=64, bufs=3)
+            dst = dealt[:].rearrange("p (t m j) -> p m j t", t=PACK, j=PACK)
             src = raw[:].rearrange("p j (m t) -> p m j t", t=PACK)
-            if scalar_m > 0:
-                nc.scalar.copy(out=dst[:, :scalar_m], in_=src[:, :scalar_m])
-            if scalar_m < P:
-                nc.vector.tensor_copy(out=dst[:, scalar_m:], in_=src[:, scalar_m:])
-            return grouped
+            if scalar_groups > 0:
+                nc.scalar.copy(out=dst[:, :scalar_groups], in_=src[:, :scalar_groups])
+            if scalar_groups < P:
+                nc.vector.tensor_copy(out=dst[:, scalar_groups:], in_=src[:, scalar_groups:])
+            return dealt
 
         def quantize(src, name):
             width = src.shape[1] // PACK
@@ -107,77 +102,96 @@ def tile_list_mask_pressure_planner_kernel(
             nc.vector.quantize_mx(out=codes[:].bitcast(FP8X4), scales=scales[:], in_=src)
             return codes, scales
 
+        v_w = [keep.tile([P, S], U32, name="v_w%d" % a, align_bytes=64) for a in range(2)]
+        v_s = keep.tile([P, S], U8, name="v_s", align_bytes=64)
         w2_w = keep.tile([P, 2 * H], U8, name="w2_w", align_bytes=64)
         w2_s = keep.tile([P, H], U8, name="w2_s", align_bytes=64)
         nc.vector.tensor_copy(
-            out=w2_w[:].rearrange("p (g t q b) -> p g t q b", g=2, t=PACK, b=2),
-            in_=w2_raw[:].rearrange("p (g q t b) -> p g t q b", g=2, t=PACK, b=2),
+            out=w2_w[:].rearrange("p (g t m b) -> p g t m b", g=2, t=PACK, b=2),
+            in_=w2_raw[:].rearrange("p (g m t b) -> p g t m b", g=2, t=PACK, b=2),
         )
         nc.vector.tensor_copy(out=v_w[0][:], in_=tab_w[0][:].bitcast(U32).indirect(offsets[:]))
         nc.vector.tensor_copy(out=v_s[:], in_=tab_s[:].indirect(offsets[:]))
         nc.vector.tensor_copy(
-            out=w2_s[:].rearrange("p (g t q) -> p g t q", g=2, t=PACK),
-            in_=w2_s_raw[:].rearrange("p (g q t) -> p g t q", g=2, t=PACK),
+            out=w2_s[:].rearrange("p (g t m) -> p g t m", g=2, t=PACK),
+            in_=w2_s_raw[:].rearrange("p (g m t) -> p g t m", g=2, t=PACK),
         )
 
         w1_q = {}
-        w1_g0 = deal(w1_raw[0], "w1_g0", P)
-        for u in range(2):
-            w1_q[0, u] = quantize(w1_g0[:, u * 2 * KP : (u + 1) * 2 * KP], "w1_0%d" % u)
-        nc.vector.tensor_copy(out=v_w[1][:], in_=tab_w[1][:].bitcast(U32).indirect(offsets[:]))
-        w1_g1 = deal(w1_raw[1], "w1_g1", W1_SCALAR_M)
-        for u in range(2):
-            w1_q[1, u] = quantize(w1_g1[:, u * 2 * KP : (u + 1) * 2 * KP], "w1_1%d" % u)
-        for a in range(2):
-            nc.sync.dma_start(w3_raw[a][:], rows_of(w3, a, 0))
 
+        def quantize_w1(a, dealt):
+            for pair in range(2):
+                w1_q[a, pair] = quantize(dealt[:, pair * 2 * KP : (pair + 1) * 2 * KP], "w1_%d%d" % (a, pair))
+
+        quantize_w1(0, deal(w1_raw[0], "w1_dealt0", P))
+        nc.vector.tensor_copy(out=v_w[1][:], in_=tab_w[1][:].bitcast(U32).indirect(offsets[:]))
+        quantize_w1(1, deal(w1_raw[1], "w1_dealt1", W1_LAST_SCALAR_GROUPS))
+
+        w3_raw = [ring.tile([P, PACK, KP], F32, name="w3_raw%d" % g, tag="w1_then_w3") for g in range(2)]
+        for g in range(2):
+            nc.sync.dma_start(w3_raw[g][:], rows_of(w3, g, 0))
 
         p_bank = {}
-        for hf in range(2):
+        for half in range(2):
             for t in range(PACK):
-                p_bank[hf, t] = psum.tile([P, HALF], F32, name="p%d%d" % (hf, t), tag="bank_s" if hf == 0 else "bank_v")
-        for hf in range(2):
-            cols = slice(hf * HALF, (hf + 1) * HALF)
+                tag = "scalar_reads" if half == 0 else "vector_reads"
+                p_bank[half, t] = psum.tile([P, HALF], F32, name="p%d%d" % (half, t), tag=tag)
+        for half in range(2):
+            cols = slice(half * HALF, (half + 1) * HALF)
             for a in range(2):
                 for t in range(PACK):
-                    m = slice(t % 2 * P, (t % 2 + 1) * P)
+                    codes, scales = w1_q[a, t // 2]
+                    places = slice(t % 2 * P, (t % 2 + 1) * P)
                     nc.tensor.matmul_mx(
-                        out=p_bank[hf, t][:],
-                        lhsT=w1_q[a, t // 2][0][:, m].bitcast(FP8X4),
-                        lhsT_scale=w1_q[a, t // 2][1][:, m],
+                        out=p_bank[half, t][:],
+                        lhsT=codes[:, places].bitcast(FP8X4),
+                        lhsT_scale=scales[:, places],
                         rhs=v_w[a][:, cols].bitcast(FP8X4),
                         rhs_scale=v_s[4 * a : P, cols],
                         start=(a == 0),
                         stop=(a == 1),
                     )
-
-        def tanh_half(hf):
-            th = ring.tile([P, PACK, HALF], F32, name="th%d" % hf, tag="th_y")
+        bounded = []
+        for half in range(2):
+            bounded.append(ring.tile([P, PACK, HALF], F32, name="bounded%d" % half, tag="bounded"))
             for t in range(PACK):
-                nc.scalar.activation(out=th[:, t, :], in_=p_bank[hf, t][:], func=ACT.Tanh, bias=b1_t[:, t : t + 1])
-            return th
+                nc.scalar.activation(
+                    out=bounded[half][:, t, :], in_=p_bank[half, t][:], func=ACT.Tanh, bias=b1_t[:, t : t + 1]
+                )
 
-        def gain_quarter(qt):
-            hb = ring.tile([P, PACK * QUARTER], BF16, name="hb%d" % qt, tag="hb", align_bytes=64, bufs=3)
-            cols = slice(qt % 2 * QUARTER, (qt % 2 + 1) * QUARTER)
+        def gain_quarter(quarter):
+            h_tile = ring.tile([P, PACK * QUARTER], BF16, name="h%d" % quarter, tag="h", align_bytes=64, bufs=3)
+            cols = slice(quarter % 2 * QUARTER, (quarter % 2 + 1) * QUARTER)
             nc.vector.tensor_tensor(
-                out=hb[:].rearrange("p (c i t) -> p c t i", i=4, t=PACK),
-                in0=th[qt // 2][:, :, cols].rearrange("p t (c i) -> p c t i", i=4),
-                in1=gain_t[:].unsqueeze(1).unsqueeze(3).to_broadcast([P, QUARTER // 4, PACK, 4]),
+                out=h_tile[:].rearrange("p (c i t) -> p c t i", i=LINE, t=PACK),
+                in0=bounded[quarter // 2][:, :, cols].rearrange("p t (c i) -> p c t i", i=LINE),
+                in1=gain_t[:].unsqueeze(1).unsqueeze(3).to_broadcast([P, QUARTER // LINE, PACK, LINE]),
                 op=ALU.mult,
             )
-            return hb
+            return h_tile
 
-        def product_a(g, c, tag):
-            bank = psum.tile([P, PACK, CH], F32, name="a%d%d" % (g, c), tag=tag)
-            codes, scales = h_q[c * CH // QUARTER]
-            cols = slice(c * CH % QUARTER, c * CH % QUARTER + CH)
+        wx_q = {}
+        h_q = []
+        h_woven = []
+        for step, (a, g) in enumerate(wx_tiles):
+            shared = 0 < step < len(wx_tiles) - 1
+            wx_dealt = deal(wx_raw[a, g], "wx_dealt%d%d" % (a, g), SHARED_SCALAR_GROUPS if shared else 0)
+            if step > 0:
+                h_q.append(quantize(h_woven[step - 1][:], "h%d" % (step - 1)))
+            h_woven.append(gain_quarter(step))
+            wx_q[a, g] = quantize(wx_dealt[:], "wx%d%d" % (a, g))
+        h_q.append(quantize(h_woven[-1][:], "h3"))
+
+        def profile_sum(g, c, tag):
+            bank = psum.tile([P, PACK, CHUNK], F32, name="profile%d%d" % (g, c), tag=tag)
+            codes, scales = h_q[c * CHUNK // QUARTER]
+            cols = slice(c * CHUNK % QUARTER, c * CHUNK % QUARTER + CHUNK)
             for t in range(PACK):
-                s = g * PACK + t
+                first = (g * PACK + t) * P
                 nc.tensor.matmul_mx(
                     out=bank[:, t, :],
-                    lhsT=w2_w[:, 2 * s * P : 2 * (s + 1) * P].bitcast(FP4X4),
-                    lhsT_scale=w2_s[:, s * P : (s + 1) * P],
+                    lhsT=w2_w[:, 2 * first : 2 * (first + P)].bitcast(FP4X4),
+                    lhsT_scale=w2_s[:, first : first + P],
                     rhs=codes[:, cols].bitcast(FP8X4),
                     rhs_scale=scales[:, cols],
                     start=True,
@@ -185,16 +199,17 @@ def tile_list_mask_pressure_planner_kernel(
                 )
             return bank
 
-        def product_b(g, c, tag):
-            bank = psum.tile([P, PACK, CH], F32, name="b%d%d" % (g, c), tag=tag)
-            cols = slice(c * CH, (c + 1) * CH)
+        def demand_sum(g, c, tag):
+            bank = psum.tile([P, PACK, CHUNK], F32, name="demand%d%d" % (g, c), tag=tag)
+            cols = slice(c * CHUNK, (c + 1) * CHUNK)
             for t in range(PACK):
-                m = slice(t * P, (t + 1) * P)
+                places = slice(t * P, (t + 1) * P)
                 for a in range(2):
+                    codes, scales = wx_q[a, g]
                     nc.tensor.matmul_mx(
                         out=bank[:, t, :],
-                        lhsT=wx_q[a, g][0][:, m].bitcast(FP8X4),
-                        lhsT_scale=wx_q[a, g][1][:, m],
+                        lhsT=codes[:, places].bitcast(FP8X4),
+                        lhsT_scale=scales[:, places],
                         rhs=xs_w[a][:, cols].bitcast(FP8X4),
                         rhs_scale=xs_s[4 * a : P, cols],
                         start=(a == 0),
@@ -202,110 +217,96 @@ def tile_list_mask_pressure_planner_kernel(
                     )
             return bank
 
-        def park(bank, g, c):
-            held = keep.tile([P, PACK * CH], F32, name="held%d%d" % (g, c))
-            nc.scalar.copy(out=held[:].rearrange("p (n t) -> p n t", t=PACK), in_=bank[:].rearrange("p t n -> p n t"))
-            return held
-
-        def lower(bank, parked, zb, g):
-            nc.vector.tensor_tensor(
-                out=zb[:, g, :].rearrange("p (n t) -> p n t", t=PACK),
-                in0=bank[:].rearrange("p t n -> p n t"),
-                in1=parked[:].rearrange("p (n t) -> p n t", t=PACK),
-                op=ALU.min,
-            )
-
-        wx_q = {}
-        h_q = {}
-        th = [tanh_half(0), tanh_half(1)]
-        wx_g = deal(wx_raw[0, 0], "wx_g00", 0)
-        wx_q[0, 0] = quantize(wx_g[:], "wx00")
-        hb0 = gain_quarter(0)
-        wx_g = deal(wx_raw[1, 0], "wx_g10", WX_SCALAR_M)
-        h_q[0] = quantize(hb0[:], "h0")
-        hb1 = gain_quarter(1)
-        wx_q[1, 0] = quantize(wx_g[:], "wx10")
-        h_q[1] = quantize(hb1[:], "h1")
-        hb2 = gain_quarter(2)
-        wx_g = deal(wx_raw[0, 1], "wx_g01", WX_SCALAR_M)
-        h_q[2] = quantize(hb2[:], "h2")
-        hb3 = gain_quarter(3)
-        wx_q[0, 1] = quantize(wx_g[:], "wx01")
-        h_q[3] = quantize(hb3[:], "h3")
-        wx_g = deal(wx_raw[1, 1], "wx_g11", 0)
-        wx_q[1, 1] = quantize(wx_g[:], "wx11")
-
-        held = {}
+        parked_sum = [demand_sum, profile_sum]
+        read_sum = [profile_sum, demand_sum]
+        parked = {}
 
         def park_chunk(c):
-            held[0, c] = park(product_b(0, c, "bank_s"), 0, c)
-            held[1, c] = park(product_a(1, c, "bank_s"), 1, c)
+            for g in range(2):
+                bank = parked_sum[g](g, c, "scalar_reads")
+                parked[g, c] = keep.tile([P, PACK * CHUNK], F32, name="parked%d%d" % (g, c))
+                nc.scalar.copy(
+                    out=parked[g, c][:].rearrange("p (n t) -> p n t", t=PACK), in_=bank[:].rearrange("p t n -> p n t")
+                )
 
         def lower_chunk(c):
-            zb = ring.tile([P, 2, PACK * CH], BF16, name="zb%d" % c, tag="zb", align_bytes=64, bufs=3)
-            lower(product_a(0, c, "bank_v"), held[0, c], zb, 0)
-            lower(product_b(1, c, "bank_v"), held[1, c], zb, 1)
-            return zb
+            z_tile = ring.tile([P, 2, PACK * CHUNK], BF16, name="z%d" % c, tag="z", align_bytes=64, bufs=3)
+            for g in range(2):
+                bank = read_sum[g](g, c, "vector_reads")
+                nc.vector.tensor_tensor(
+                    out=z_tile[:, g, :].rearrange("p (n t) -> p n t", t=PACK),
+                    in0=bank[:].rearrange("p t n -> p n t"),
+                    in1=parked[g, c][:].rearrange("p (n t) -> p n t", t=PACK),
+                    op=ALU.min,
+                )
+            return z_tile
 
         for c in range(PARK_AHEAD):
             park_chunk(c)
-        w3_q = [quantize(deal(w3_raw[a], "w3_g%d" % a, P if a == 0 else WX_SCALAR_M)[:], "w3_%d" % a) for a in range(2)]
+        w3_q = [
+            quantize(deal(w3_raw[g], "w3_dealt%d" % g, SHARED_SCALAR_GROUPS if g == 1 else P)[:], "w3_%d" % g)
+            for g in range(2)
+        ]
 
         y_w = keep.tile([P, S], U32, name="y_w", align_bytes=64)
         y_s = keep.tile([P, S], U8, name="y_s", align_bytes=64)
         out_rows = out_0.rearrange("(p t) s -> p t s", t=PACK)
         out_words = words_of(out_1, 0)
 
-        def finish(c):
-            cols = slice(c * CH, (c + 1) * CH)
-            bank = psum.tile([P, PACK, CH], F32, name="y%d" % c, tag="bank_s")
+        def last_product(c):
+            bank = psum.tile([P, PACK, CHUNK], F32, name="y%d" % c, tag="scalar_reads")
+            z_codes, z_scales = z_q[c]
             for t in range(PACK):
-                m = slice(t * P, (t + 1) * P)
+                places = slice(t * P, (t + 1) * P)
                 for g in range(2):
+                    codes, scales = w3_q[g]
                     nc.tensor.matmul_mx(
                         out=bank[:, t, :],
-                        lhsT=w3_q[g][0][:, m].bitcast(FP8X4),
-                        lhsT_scale=w3_q[g][1][:, m],
-                        rhs=z_q[c][0][:, g * CH : (g + 1) * CH].bitcast(FP8X4),
-                        rhs_scale=z_q[c][1][:, g * CH : (g + 1) * CH],
+                        lhsT=codes[:, places].bitcast(FP8X4),
+                        lhsT_scale=scales[:, places],
+                        rhs=z_codes[:, g * CHUNK : (g + 1) * CHUNK].bitcast(FP8X4),
+                        rhs_scale=z_scales[:, g * CHUNK : (g + 1) * CHUNK],
                         start=(g == 0),
                         stop=(g == 1),
                     )
-            yb = ring.tile([P, PACK * CH], BF16, name="yb%d" % c, tag="yb", align_bytes=64, bufs=3)
-            y32 = ring.tile([P, PACK, CH], F32, name="y32_%d" % c, tag="y32", bufs=4)
-            if c < VECTOR_ROUNDS_FROM:
-                nc.scalar.copy(out=yb[:].rearrange("p (n t) -> p n t", t=PACK), in_=bank[:].rearrange("p t n -> p n t"))
-                nc.scalar.copy(out=y32[:], in_=bank[:])
-            else:
-                nc.scalar.copy(out=y32[:], in_=bank[:])
-                nc.vector.tensor_copy(
-                    out=yb[:].rearrange("p (c i t) -> p c t i", i=4, t=PACK),
-                    in_=y32[:].rearrange("p t (c i) -> p c t i", i=4),
+            y_tile = ring.tile([P, PACK * CHUNK], BF16, name="y_woven%d" % c, tag="y_woven", align_bytes=64, bufs=3)
+            y_rows = ring.tile([P, PACK, CHUNK], F32, name="y_rows%d" % c, tag="y_rows", bufs=4)
+            if c < VECTOR_WEAVES_FROM:
+                nc.scalar.copy(
+                    out=y_tile[:].rearrange("p (n t) -> p n t", t=PACK), in_=bank[:].rearrange("p t n -> p n t")
                 )
-            nc.sync.dma_start(out_rows[:, :, cols], y32[:])
-            return yb
+                nc.scalar.copy(out=y_rows[:], in_=bank[:])
+            else:
+                nc.scalar.copy(out=y_rows[:], in_=bank[:])
+                nc.vector.tensor_copy(
+                    out=y_tile[:].rearrange("p (c i t) -> p c t i", i=LINE, t=PACK),
+                    in_=y_rows[:].rearrange("p t (c i) -> p c t i", i=LINE),
+                )
+            nc.sync.dma_start(out_rows[:, :, c * CHUNK : (c + 1) * CHUNK], y_rows[:])
+            return y_tile
 
-        def finish_planes(c, yb):
-            cols = slice(c * CH, (c + 1) * CH)
-            nc.vector.quantize_mx(out=y_w[:, cols].bitcast(FP8X4), scales=y_s[:, cols], in_=yb[:])
+        def output_planes(c):
+            cols = slice(c * CHUNK, (c + 1) * CHUNK)
+            nc.vector.quantize_mx(out=y_w[:, cols].bitcast(FP8X4), scales=y_s[:, cols], in_=y_woven[c][:])
             if c % 2 == 1:
-                both = slice((c - 1) * CH, (c + 1) * CH)
+                both = slice((c - 1) * CHUNK, (c + 1) * CHUNK)
                 nc.sync.dma_start(out_words[:, both], y_w[:, both].bitcast(I32))
 
-        zbs = {}
+        z_woven = {}
         z_q = {}
-        ybs = {}
-        for c in range(NCH + 4):
-            if c < NCH:
-                zbs[c] = lower_chunk(c)
-            if 1 <= c <= NCH:
-                z_q[c - 1] = quantize(zbs[c - 1][:].rearrange("p g w -> p (g w)"), "z%d" % (c - 1))
-            if 2 <= c < NCH + 2:
-                ybs[c - 2] = finish(c - 2)
-            if c + PARK_AHEAD < NCH:
+        y_woven = {}
+        for c in range(CHUNKS + PLANES_LAG):
+            if c < CHUNKS:
+                z_woven[c] = lower_chunk(c)
+            if 0 <= c - 1 < CHUNKS:
+                z_q[c - 1] = quantize(z_woven[c - 1][:].rearrange("p g w -> p (g w)"), "z%d" % (c - 1))
+            if 0 <= c - PRODUCT_LAG < CHUNKS:
+                y_woven[c - PRODUCT_LAG] = last_product(c - PRODUCT_LAG)
+            if c + PARK_AHEAD < CHUNKS:
                 park_chunk(c + PARK_AHEAD)
-            if c >= 4:
-                finish_planes(c - 4, ybs[c - 4])
-        for q in range(4):
+            if c >= PLANES_LAG:
+                output_planes(c - PLANES_LAG)
+
+        for q in range(QUADRANTS):
             queue = nc.sync if q % 2 == 0 else nc.scalar
             queue.dma_start(out_2[0, 4 * q : 4 * q + 4, :].bitcast(I32), y_s[32 * q : 32 * q + 4, :].bitcast(I32))

from contextlib import ExitStack

import concourse.mybir as mybir

K, R, H, N, T, S = 1024, 512, 1024, 512, 4096, 1024
FLOPS = 2 * S * (K * R + R * H + K * H + H * N)

F32 = mybir.dt.float32
BF16 = mybir.dt.bfloat16
I32 = mybir.dt.int32
U32 = mybir.dt.uint32
U16 = mybir.dt.uint16
U8 = mybir.dt.uint8
FP8X4 = mybir.dt.float8_e4m3fn_x4
FP4X4 = mybir.dt.float4_e2m1fn_x4
ACT = mybir.ActivationFunctionType
ALU = mybir.AluOpType

P = 128
PACK = 4
KP = P * PACK
QUADRANTS = 4
HALF = 512
QUARTER = 256
CHUNK = 128
CHUNKS = S // CHUNK
LINE = 4

W1_LAST_SCALAR_GROUPS = 40
SHARED_SCALAR_GROUPS = 64
PARK_AHEAD = 5
PRODUCT_LAG = 2
PLANES_LAG = 4
VECTOR_WEAVES_FROM = 6


def tile_list_mask_pressure_planner_kernel(
    tc, tab_words, tab_scales, offs, xs_words, xs_scales, w1, b1, gain, w2_words, w2_scales, wx, w3, out_0, out_1, out_2
):
    nc = tc.nc
    with ExitStack() as ctx:
        keep = ctx.enter_context(tc.tile_pool(name="keep", bufs=1))
        ring = ctx.enter_context(tc.tile_pool(name="ring", bufs=2))
        psum = ctx.enter_context(tc.psum_pool(name="psum", bufs=4))

        def words_of(dram, a):
            return dram[a].rearrange("p n t -> p (n t)").bitcast(I32)

        def rows_of(w, a, g):
            return w[a * KP : (a + 1) * KP, g * KP : (g + 1) * KP].rearrange("(p j) c -> p j c", j=PACK)

        def load_scale_rows(name, dram, passes, width):
            plane = keep.tile([P, width], U8, name=name, align_bytes=64)
            nc.vector.memset(plane[:].bitcast(I32), 0)
            for q in range(QUADRANTS):
                nc.sync.dma_start(
                    plane[32 * q : 32 * q + 4 * passes, :].bitcast(I32), dram[:, 4 * q : 4 * q + 4, :].bitcast(I32)
                )
            return plane

        offsets = keep.tile([P, S // 16], U16, name="offsets")
        nc.sync.dma_start(offsets[:], offs)
        w2_raw = keep.tile([P, 2 * H], U8, name="w2_raw")
        nc.sync.dma_start(w2_raw[:].bitcast(I32), w2_words[0].bitcast(I32))
        tab_w = [keep.tile([P, T], I32, name="tab_w%d" % a) for a in range(2)]
        w1_raw = [ring.tile([P, PACK, KP], F32, name="w1_raw%d" % a, tag="w1_then_w3") for a in range(2)]
        nc.sync.dma_start(tab_w[0][:], words_of(tab_words, 0))
        tab_s = load_scale_rows("tab_s", tab_scales, 2, T)
        nc.sync.dma_start(w1_raw[0][:], rows_of(w1, 0, 0))
        w2_s_raw = load_scale_rows("w2_s_raw", w2_scales, 1, H)
        nc.sync.dma_start(tab_w[1][:], words_of(tab_words, 1))
        nc.sync.dma_start(w1_raw[1][:], rows_of(w1, 1, 0))
        wx_tiles = [(a, g) for g in range(2) for a in range(2)]
        wx_raw = {}
        xs_w = [keep.tile([P, S], I32, name="xs_w%d" % a, align_bytes=64) for a in range(2)]
        for a, g in wx_tiles:
            wx_raw[a, g] = keep.tile([P, PACK, KP], F32, name="wx_raw%d%d" % (a, g))
            nc.sync.dma_start(wx_raw[a, g][:], rows_of(wx, a, g))
            if (a, g) == (1, 0):
                nc.sync.dma_start(xs_w[0][:], words_of(xs_words, 0))
                xs_s = load_scale_rows("xs_s", xs_scales, 2, S)
                nc.sync.dma_start(xs_w[1][:], words_of(xs_words, 1))
        b1_t = keep.tile([P, PACK], F32, name="b1_t")
        gain_t = keep.tile([P, PACK], F32, name="gain_t")
        nc.gpsimd.dma_start(b1_t[:], b1.rearrange("(p t) -> p t", t=PACK))
        nc.gpsimd.dma_start(gain_t[:], gain.rearrange("(p t) -> p t", t=PACK))

        def deal(raw, name, scalar_groups):
            dealt = ring.tile([P, PACK * KP], BF16, name=name, tag="dealt", align_bytes=64, bufs=3)
            dst = dealt[:].rearrange("p (t m j) -> p m j t", t=PACK, j=PACK)
            src = raw[:].rearrange("p j (m t) -> p m j t", t=PACK)
            if scalar_groups > 0:
                nc.scalar.copy(out=dst[:, :scalar_groups], in_=src[:, :scalar_groups])
            if scalar_groups < P:
                nc.vector.tensor_copy(out=dst[:, scalar_groups:], in_=src[:, scalar_groups:])
            return dealt

        def quantize(src, name):
            width = src.shape[1] // PACK
            codes = keep.tile([P, width], U32, name=name + "_w", align_bytes=64)
            scales = keep.tile([P, width], U8, name=name + "_s", align_bytes=64)
            nc.vector.quantize_mx(out=codes[:].bitcast(FP8X4), scales=scales[:], in_=src)
            return codes, scales

        v_w = [keep.tile([P, S], U32, name="v_w%d" % a, align_bytes=64) for a in range(2)]
        v_s = keep.tile([P, S], U8, name="v_s", align_bytes=64)
        w2_w = keep.tile([P, 2 * H], U8, name="w2_w", align_bytes=64)
        w2_s = keep.tile([P, H], U8, name="w2_s", align_bytes=64)
        nc.vector.tensor_copy(
            out=w2_w[:].rearrange("p (g t m b) -> p g t m b", g=2, t=PACK, b=2),
            in_=w2_raw[:].rearrange("p (g m t b) -> p g t m b", g=2, t=PACK, b=2),
        )
        nc.vector.tensor_copy(out=v_w[0][:], in_=tab_w[0][:].bitcast(U32).indirect(offsets[:]))
        nc.vector.tensor_copy(out=v_s[:], in_=tab_s[:].indirect(offsets[:]))
        nc.vector.tensor_copy(
            out=w2_s[:].rearrange("p (g t m) -> p g t m", g=2, t=PACK),
            in_=w2_s_raw[:].rearrange("p (g m t) -> p g t m", g=2, t=PACK),
        )

        w1_q = {}

        def quantize_w1(a, dealt):
            for pair in range(2):
                w1_q[a, pair] = quantize(dealt[:, pair * 2 * KP : (pair + 1) * 2 * KP], "w1_%d%d" % (a, pair))

        quantize_w1(0, deal(w1_raw[0], "w1_dealt0", P))
        nc.vector.tensor_copy(out=v_w[1][:], in_=tab_w[1][:].bitcast(U32).indirect(offsets[:]))
        quantize_w1(1, deal(w1_raw[1], "w1_dealt1", W1_LAST_SCALAR_GROUPS))

        w3_raw = [ring.tile([P, PACK, KP], F32, name="w3_raw%d" % g, tag="w1_then_w3") for g in range(2)]
        for g in range(2):
            nc.sync.dma_start(w3_raw[g][:], rows_of(w3, g, 0))

        p_bank = {}
        for half in range(2):
            for t in range(PACK):
                tag = "scalar_reads" if half == 0 else "vector_reads"
                p_bank[half, t] = psum.tile([P, HALF], F32, name="p%d%d" % (half, t), tag=tag)
        for half in range(2):
            cols = slice(half * HALF, (half + 1) * HALF)
            for a in range(2):
                for t in range(PACK):
                    codes, scales = w1_q[a, t // 2]
                    places = slice(t % 2 * P, (t % 2 + 1) * P)
                    nc.tensor.matmul_mx(
                        out=p_bank[half, t][:],
                        lhsT=codes[:, places].bitcast(FP8X4),
                        lhsT_scale=scales[:, places],
                        rhs=v_w[a][:, cols].bitcast(FP8X4),
                        rhs_scale=v_s[4 * a : P, cols],
                        start=(a == 0),
                        stop=(a == 1),
                    )
        bounded = []
        for half in range(2):
            bounded.append(ring.tile([P, PACK, HALF], F32, name="bounded%d" % half, tag="bounded"))
            for t in range(PACK):
                nc.scalar.activation(
                    out=bounded[half][:, t, :], in_=p_bank[half, t][:], func=ACT.Tanh, bias=b1_t[:, t : t + 1]
                )

        def gain_quarter(quarter):
            h_tile = ring.tile([P, PACK * QUARTER], BF16, name="h%d" % quarter, tag="h", align_bytes=64, bufs=3)
            cols = slice(quarter % 2 * QUARTER, (quarter % 2 + 1) * QUARTER)
            nc.vector.tensor_tensor(
                out=h_tile[:].rearrange("p (c i t) -> p c t i", i=LINE, t=PACK),
                in0=bounded[quarter // 2][:, :, cols].rearrange("p t (c i) -> p c t i", i=LINE),
                in1=gain_t[:].unsqueeze(1).unsqueeze(3).to_broadcast([P, QUARTER // LINE, PACK, LINE]),
                op=ALU.mult,
            )
            return h_tile

        wx_q = {}
        h_q = []
        h_woven = []
        for step, (a, g) in enumerate(wx_tiles):
            shared = 0 < step < len(wx_tiles) - 1
            wx_dealt = deal(wx_raw[a, g], "wx_dealt%d%d" % (a, g), SHARED_SCALAR_GROUPS if shared else 0)
            if step > 0:
                h_q.append(quantize(h_woven[step - 1][:], "h%d" % (step - 1)))
            h_woven.append(gain_quarter(step))
            wx_q[a, g] = quantize(wx_dealt[:], "wx%d%d" % (a, g))
        h_q.append(quantize(h_woven[-1][:], "h3"))

        def profile_sum(g, c, tag):
            bank = psum.tile([P, PACK, CHUNK], F32, name="profile%d%d" % (g, c), tag=tag)
            codes, scales = h_q[c * CHUNK // QUARTER]
            cols = slice(c * CHUNK % QUARTER, c * CHUNK % QUARTER + CHUNK)
            for t in range(PACK):
                first = (g * PACK + t) * P
                nc.tensor.matmul_mx(
                    out=bank[:, t, :],
                    lhsT=w2_w[:, 2 * first : 2 * (first + P)].bitcast(FP4X4),
                    lhsT_scale=w2_s[:, first : first + P],
                    rhs=codes[:, cols].bitcast(FP8X4),
                    rhs_scale=scales[:, cols],
                    start=True,
                    stop=True,
                )
            return bank

        def demand_sum(g, c, tag):
            bank = psum.tile([P, PACK, CHUNK], F32, name="demand%d%d" % (g, c), tag=tag)
            cols = slice(c * CHUNK, (c + 1) * CHUNK)
            for t in range(PACK):
                places = slice(t * P, (t + 1) * P)
                for a in range(2):
                    codes, scales = wx_q[a, g]
                    nc.tensor.matmul_mx(
                        out=bank[:, t, :],
                        lhsT=codes[:, places].bitcast(FP8X4),
                        lhsT_scale=scales[:, places],
                        rhs=xs_w[a][:, cols].bitcast(FP8X4),
                        rhs_scale=xs_s[4 * a : P, cols],
                        start=(a == 0),
                        stop=(a == 1),
                    )
            return bank

        parked_sum = [demand_sum, profile_sum]
        read_sum = [profile_sum, demand_sum]
        parked = {}

        def park_chunk(c):
            for g in range(2):
                bank = parked_sum[g](g, c, "scalar_reads")
                parked[g, c] = keep.tile([P, PACK * CHUNK], F32, name="parked%d%d" % (g, c))
                nc.scalar.copy(
                    out=parked[g, c][:].rearrange("p (n t) -> p n t", t=PACK), in_=bank[:].rearrange("p t n -> p n t")
                )

        def lower_chunk(c):
            z_tile = ring.tile([P, 2, PACK * CHUNK], BF16, name="z%d" % c, tag="z", align_bytes=64, bufs=3)
            for g in range(2):
                bank = read_sum[g](g, c, "vector_reads")
                nc.vector.tensor_tensor(
                    out=z_tile[:, g, :].rearrange("p (n t) -> p n t", t=PACK),
                    in0=bank[:].rearrange("p t n -> p n t"),
                    in1=parked[g, c][:].rearrange("p (n t) -> p n t", t=PACK),
                    op=ALU.min,
                )
            return z_tile

        for c in range(PARK_AHEAD):
            park_chunk(c)
        w3_q = [
            quantize(deal(w3_raw[g], "w3_dealt%d" % g, SHARED_SCALAR_GROUPS if g == 1 else P)[:], "w3_%d" % g)
            for g in range(2)
        ]

        y_w = keep.tile([P, S], U32, name="y_w", align_bytes=64)
        y_s = keep.tile([P, S], U8, name="y_s", align_bytes=64)
        out_rows = out_0.rearrange("(p t) s -> p t s", t=PACK)
        out_words = words_of(out_1, 0)

        def last_product(c):
            bank = psum.tile([P, PACK, CHUNK], F32, name="y%d" % c, tag="scalar_reads")
            z_codes, z_scales = z_q[c]
            for t in range(PACK):
                places = slice(t * P, (t + 1) * P)
                for g in range(2):
                    codes, scales = w3_q[g]
                    nc.tensor.matmul_mx(
                        out=bank[:, t, :],
                        lhsT=codes[:, places].bitcast(FP8X4),
                        lhsT_scale=scales[:, places],
                        rhs=z_codes[:, g * CHUNK : (g + 1) * CHUNK].bitcast(FP8X4),
                        rhs_scale=z_scales[:, g * CHUNK : (g + 1) * CHUNK],
                        start=(g == 0),
                        stop=(g == 1),
                    )
            y_tile = ring.tile([P, PACK * CHUNK], BF16, name="y_woven%d" % c, tag="y_woven", align_bytes=64, bufs=3)
            y_rows = ring.tile([P, PACK, CHUNK], F32, name="y_rows%d" % c, tag="y_rows", bufs=4)
            if c < VECTOR_WEAVES_FROM:
                nc.scalar.copy(
                    out=y_tile[:].rearrange("p (n t) -> p n t", t=PACK), in_=bank[:].rearrange("p t n -> p n t")
                )
                nc.scalar.copy(out=y_rows[:], in_=bank[:])
            else:
                nc.scalar.copy(out=y_rows[:], in_=bank[:])
                nc.vector.tensor_copy(
                    out=y_tile[:].rearrange("p (c i t) -> p c t i", i=LINE, t=PACK),
                    in_=y_rows[:].rearrange("p t (c i) -> p c t i", i=LINE),
                )
            nc.sync.dma_start(out_rows[:, :, c * CHUNK : (c + 1) * CHUNK], y_rows[:])
            return y_tile

        def output_planes(c):
            cols = slice(c * CHUNK, (c + 1) * CHUNK)
            nc.vector.quantize_mx(out=y_w[:, cols].bitcast(FP8X4), scales=y_s[:, cols], in_=y_woven[c][:])
            if c % 2 == 1:
                both = slice((c - 1) * CHUNK, (c + 1) * CHUNK)
                nc.sync.dma_start(out_words[:, both], y_w[:, both].bitcast(I32))

        z_woven = {}
        z_q = {}
        y_woven = {}
        for c in range(CHUNKS + PLANES_LAG):
            if c < CHUNKS:
                z_woven[c] = lower_chunk(c)
            if 0 <= c - 1 < CHUNKS:
                z_q[c - 1] = quantize(z_woven[c - 1][:].rearrange("p g w -> p (g w)"), "z%d" % (c - 1))
            if 0 <= c - PRODUCT_LAG < CHUNKS:
                y_woven[c - PRODUCT_LAG] = last_product(c - PRODUCT_LAG)
            if c + PARK_AHEAD < CHUNKS:
                park_chunk(c + PARK_AHEAD)
            if c >= PLANES_LAG:
                output_planes(c - PLANES_LAG)

        for q in range(QUADRANTS):
            queue = nc.sync if q % 2 == 0 else nc.scalar
            queue.dma_start(out_2[0, 4 * q : 4 * q + 4, :].bitcast(I32), y_s[32 * q : 32 * q + 4, :].bitcast(I32))
